import numpy as np
import ml_dtypes


def mxq(x, axis, fmt="e4m3"):
    dtype, down = {"e4m3": (ml_dtypes.float8_e4m3fn, 7), "e5m2": (ml_dtypes.float8_e5m2, 14)}[fmt]
    v = np.moveaxis(np.asarray(x, np.float32).astype(ml_dtypes.bfloat16).astype(np.float64), axis, -1)
    blocks = v.reshape(v.shape[:-1] + (-1, 32))
    amax = np.abs(blocks).max(-1, keepdims=True)
    byte = np.maximum(np.where(amax > 0, np.frexp(amax)[1] - 1 + 127, 0) - down, 1)
    scale = np.exp2(byte - 127.0)
    codes = (blocks / scale).astype(np.float32).astype(dtype).astype(np.float64)
    return np.moveaxis((codes * scale).reshape(v.shape), -1, axis)


WIDE = False


def mx_kscale(k):
    if not WIDE:
        return np.ones(k)
    levels = np.array([10, -10, 5, -5, 0])
    if k % 512:
        return np.exp2(np.random.permutation(np.resize(levels, k // 32))).repeat(32)
    a = np.empty((k // 512, 16))
    for p in range(k // 512):
        a[p, :8] = np.random.permutation(np.resize(levels, 8))
        for g in range(8):
            far = levels[np.abs(levels - a[p, g]) >= 10]
            a[p, g + 8] = far[np.random.randint(len(far))]
    return np.exp2(a.ravel()).repeat(32)


BF16 = ml_dtypes.bfloat16


def bf(x):
    return np.asarray(x, np.float32).astype(BF16)


def f64(x):
    return np.asarray(x).astype(np.float64)


B, Z, H, C, L, A = 1024, 512, 1024, 512, 64, 20
O = L * A


def sigmoid(v):
    return 1.0 / (1.0 + np.exp(-v))


def _gated_output_weight(w, s, dictionary):
    ws = w * sigmoid(s)
    return mxq(ws, 1, "e4m3") @ mxq(dictionary, 0, "e4m3")


def _log_normalize(logits):
    m = logits.max(-1, keepdims=True)
    return logits - (m + np.log(np.sum(np.exp(logits - m), axis=-1, keepdims=True)))


def draw0():
    p, t, u = mx_kscale(Z), mx_kscale(H), mx_kscale(C)
    return {
        "z": bf(np.random.standard_normal((B, Z)) * p),
        "w1": bf(np.random.standard_normal((Z, H)) / np.sqrt(Z) / p[:, None] * t),
        "b1": bf(np.random.standard_normal(H) * 0.3 * t),
        "w": bf(np.random.standard_normal((H, C)) * 4.0 / np.sqrt(H) / t[:, None] * u),
        "s": bf(np.random.standard_normal((H, C))),
        "dict": bf(np.random.standard_normal((C, O)) / np.sqrt(C) / u[:, None]),
        "b": bf(np.random.standard_normal(O) * 0.5),
    }


def core(z, w1, b1, w, s, dict, b):
    h = np.maximum((mxq(f64(z), 1, "e4m3") @ mxq(f64(w1), 0, "e4m3")) + f64(b1), 0.0)
    weff = _gated_output_weight(f64(w), f64(s), f64(dict))
    logits = (mxq(h, 1, "e4m3") @ mxq(weff, 0, "e4m3")) + f64(b)
    logits = np.reshape(logits, (z.shape[0], L, A))
    return _log_normalize(logits)


def e4m3fn_bytes(y):
    return np.clip(np.asarray(y, np.float64), -448.0, 448.0).astype(np.float32).astype(ml_dtypes.float8_e4m3fn).view(np.uint8)


def e4m3fn_values(b):
    return np.asarray(b, np.uint8).view(ml_dtypes.float8_e4m3fn).astype(np.float64)


def setup_inputs():
    d = draw0()
    x0 = np.asarray(d['dict']).astype(np.float64)
    s = (np.max(np.abs(x0), axis=(1,), keepdims=True) / 448.0).astype(np.float32)
    out = {}
    for k, v in d.items():
        if k == 'dict':
            out['dict_bytes'] = e4m3fn_bytes(x0 / s.astype(np.float64))
            out['dict_scale'] = s
        else:
            out[k] = v
    return out


def reference(z, w1, b1, w, s, dict_bytes, dict_scale, b):
    return core(z, w1, b1, w, s, e4m3fn_values(dict_bytes) * dict_scale.astype(np.float64), b)

@@ -1,0 +1,476 @@
+from contextlib import ExitStack
+
+import concourse.mybir as mybir
+from concourse.masks import make_identity
+
+B, Z, H, C, L, A = 1024, 512, 1024, 512, 64, 20
+O = L * A
+FLOPS = 2 * (B * Z * H + H * C * O + B * H * O)
+
+F32 = mybir.dt.float32
+BF16 = mybir.dt.bfloat16
+U32 = mybir.dt.uint32
+U8 = mybir.dt.uint8
+FP8 = mybir.dt.float8_e4m3fn
+FP8X4 = mybir.dt.float8_e4m3fn_x4
+ALU = mybir.AluOpType
+ACT = mybir.ActivationFunctionType
+AXIS = mybir.AxisListType
+
+P = 128
+PACK = 4
+BANK = 512
+CH = 256
+N_CH = B // CH
+PAIRS = A // 2
+XB = PAIRS // 2
+GPB = 6
+N_BLK = (L + GPB - 1) // GPB
+PIECES = ((0, 4), (4, 8), (8, 11))
+
+
+def tile_gateddictionaryproteinprofiledecoder_kernel(tc, z, w1, b1, w, s, dict_bytes, dict_scale, b, out):
+    nc = tc.nc
+
+    with ExitStack() as ctx:
+        sb = ctx.enter_context(tc.tile_pool(name="sb", bufs=1))
+        ps = ctx.enter_context(tc.psum_pool(name="ps", bufs=1))
+
+        def new(name, width, dtype, bufs=1):
+            return sb.tile([P, width], dtype, name=name, tag=name, bufs=bufs, align_bytes=64)
+
+        def bank(index):
+            return ps.tile([P, BANK], F32, name="bank%d" % index, tag="bank%d" % index)
+
+        def quantize(codes, scales, values, first, count):
+            nc.vector.quantize_mx(
+                out=codes[:, first : first + count].bitcast(FP8X4),
+                scales=scales[:, first : first + count],
+                in_=values,
+            )
+
+        def matmul(acc, lhs, lhs_first, rhs, rhs_first, count, start, stop):
+            nc.tensor.matmul_mx(
+                out=acc,
+                lhsT=lhs[0][:, lhs_first : lhs_first + P].bitcast(FP8X4),
+                lhsT_scale=lhs[1][:, lhs_first : lhs_first + P],
+                rhs=rhs[0][:, rhs_first : rhs_first + count].bitcast(FP8X4),
+                rhs_scale=rhs[1][:, rhs_first : rhs_first + count],
+                start=start,
+                stop=stop,
+            )
+
+        ident = new("ident", P, F32)
+        make_identity(nc, ident[:])
+
+        ctx.enter_context(tc.manual_schedule())
+
+        s_rows = s.rearrange("(g m u i) k -> g u m (i k)", g=2, u=2, i=2)
+        w_rows = w.rearrange("(g m u i) k -> g u m (i k)", g=2, u=2, i=2)
+        d_rows = dict_bytes.rearrange("(p t) n -> p t n", t=PACK)
+        z_rows = z.rearrange("(c p i) k -> c p (i k)", p=P, i=2)
+        out_rows = out.rearrange("(c p i) l a -> c i p (l a)", p=P, i=2)
+
+        s_raw = [new("s_raw%d" % q, 2 * C, BF16) for q in range(4)]
+        w_raw = [new("w_raw%d" % q, 2 * C, BF16) for q in range(4)]
+        piece_cols = [(GPB * A * b0, min(GPB * A * b1e, O)) for b0, b1e in PIECES]
+        d_raw = [new("dict_raw%d" % r, PACK * (c1 - c0), U8) for r, (c0, c1) in enumerate(piece_cols)]
+        d_scale = new("d_scale", PACK, F32)
+        w1_raw = new("w1_raw", PACK * H, BF16)
+        z_raw = [new("z_raw%d" % c, 2 * Z, BF16) for c in range(N_CH)]
+        b1_col = new("b1_col", 8, BF16)
+        b_col = new("b_col", A, BF16)
+
+        def load_gate(q):
+            nc.sync.dma_start(out=s_raw[q][:], in_=s_rows[q // 2, q % 2])
+
+        def load_w(q):
+            nc.sync.dma_start(out=w_raw[q][:], in_=w_rows[q // 2, q % 2])
+
+        def load_dict(r):
+            c0, c1 = piece_cols[r]
+            nc.sync.dma_start(out=d_raw[r][:].rearrange("p (t n) -> p t n", t=PACK), in_=d_rows[:, :, c0:c1])
+
+        load_gate(0)
+        nc.sync.dma_start(out=d_scale[:], in_=dict_scale.rearrange("(p t) o -> p (t o)", t=PACK))
+        load_w(0)
+        load_dict(0)
+        load_gate(1)
+        load_w(1)
+        load_dict(1)
+        load_gate(2)
+        load_w(2)
+        load_dict(2)
+        load_gate(3)
+        load_w(3)
+        nc.sync.dma_start(out=w1_raw[:], in_=w1.rearrange("(p j) c -> p (j c)", j=PACK))
+        nc.sync.dma_start(out=z_raw[0][:], in_=z_rows[0])
+        nc.sync.dma_start(
+            out=b1_col[:].rearrange("p (g t) -> p g t", t=PACK), in_=b1.rearrange("(g p t) -> p g t", p=P, t=PACK)
+        )
+        b_rows = b.rearrange("(g a) -> g a", a=A)
+        nc.sync.dma_start(out=b_col[0:L, :], in_=b_rows)
+        nc.sync.dma_start(out=b_col[L:P, 0 : A - 1], in_=b_rows[:, 1:A])
+        for c in range(1, N_CH):
+            nc.sync.dma_start(out=z_raw[c][:], in_=z_rows[c])
+
+        d_bf = [new("d_bf%d" % r, (b1e - b0) * BANK, BF16) for r, (b0, b1e) in enumerate(PIECES)]
+        d_mx = (new("d_codes", N_BLK * P, U32), new("d_scales", N_BLK * P, U8))
+        ws_t = [new("ws_t%d" % g, 4 * BANK, BF16) for g in range(2)]
+        ws_mx = (new("ws_codes", H, U32), new("ws_scales", H, U8))
+        w1_t = new("w1_t", PACK * H, BF16)
+        w1_mx = (new("w1_codes", H, U32), new("w1_scales", H, U8))
+        weff = [new("weff%d" % g, PACK * O, BF16) for g in range(2)]
+        weff_mx = [(new("weff_codes%d" % g, O, U32), new("weff_scales%d" % g, O, U8)) for g in range(2)]
+        z_mx = [(new("z_codes%d" % c, CH, U32), new("z_scales%d" % c, CH, U8)) for c in range(N_CH)]
+        d_spread = new("d_spread", PACK * GPB * A, F32)
+        gate = {}
+        gated = {}
+
+        def groups_in(blk):
+            return min(GPB, L - GPB * blk)
+
+        def sigmoid(q):
+            gate[q] = new("gate", 2 * C, F32, bufs=3)
+            nc.scalar.activation(out=gate[q][:], in_=s_raw[q][:], func=ACT.Sigmoid)
+
+        def gate_product(q):
+            gated[q] = new("gated", 2 * C, BF16, bufs=2)
+            nc.vector.tensor_tensor(out=gated[q][:], in0=w_raw[q][:], in1=gate[q][:], op=ALU.mult)
+
+        def turn(rows, index):
+            words = rows[:].bitcast(F32)
+            acc = bank(index)
+            for i in range(2):
+                for u in range(2):
+                    col = (2 * i + u) * P
+                    nc.tensor.transpose(acc[:, col : col + P], words[:, 256 * i + u : 256 * (i + 1) : 2], ident[:])
+            return acc
+
+        def turned_out(acc, dst):
+            nc.scalar.copy(
+                out=dst.bitcast(F32).rearrange("p (i r u) -> p i r u", i=2, u=2),
+                in_=acc[:].rearrange("p (i u r) -> p i r u", i=2, u=2),
+            )
+
+        def widen(r, blk0, blk1):
+            first = PIECES[r][0]
+            codes = d_raw[r][:].bitcast(FP8).rearrange("p (t n) -> p n t", t=PACK)
+            for blk in range(blk0, blk1):
+                cols = A * groups_in(blk)
+                c0 = (blk - first) * GPB * A
+                x0 = (blk - first) * BANK
+                nc.vector.tensor_tensor(
+                    out=d_bf[r][:, x0 : x0 + PACK * cols].rearrange("p (n t) -> p n t", t=PACK),
+                    in0=codes[:, c0 : c0 + cols, :],
+                    in1=d_spread[:, 0 : PACK * cols].rearrange("p (n t) -> p n t", t=PACK),
+                    op=ALU.mult,
+                )
+
+        def quantize_dict(r):
+            b0, b1e = PIECES[r]
+            quantize(d_mx[0], d_mx[1], d_bf[r][:], b0 * P, (b1e - b0) * P)
+
+        def expand(g, blk, index):
+            acc = bank(index)
+            for t in range(PACK):
+                matmul(acc[:, t * P : (t + 1) * P], ws_mx, (g * PACK + t) * P, d_mx, blk * P, P, True, True)
+            ng = groups_in(blk)
+            src = acc[:].rearrange("p (t n) -> p t n", t=PACK)[:, :, 0 : ng * A].rearrange("p t (g a) -> p a g t", a=A)
+            dst = weff[g][:].rearrange("p (a g t) -> p a g t", a=A, t=PACK)[:, :, GPB * blk : GPB * blk + ng, :]
+            nc.scalar.copy(out=dst, in_=src)
+
+        def interleave_w1(g):
+            nc.vector.tensor_copy(
+                out=w1_t[:, g * 2048 : (g + 1) * 2048].rearrange("p (t m i j) -> p m t i j", t=PACK, i=2, j=PACK),
+                in_=w1_raw[:]
+                .rearrange("p (j c) -> p j c", j=PACK)[:, :, g * 512 : (g + 1) * 512]
+                .rearrange("p j (m i t) -> p m t i j", i=2, t=PACK),
+            )
+
+        z_t = {}
+
+        def turn_z(c, index):
+            acc = turn(z_raw[c], index)
+            z_t[c] = new("z_t", 2 * Z, BF16, bufs=2)
+            turned_out(acc, z_t[c][:])
+
+        def quantize_z(c):
+            quantize(z_mx[c][0], z_mx[c][1], z_t[c][:], 0, CH)
+
+        h_planes = {}
+        h_words = {}
+        h_mx = {}
+
+        def hidden(c, q, index):
+            g = q // 2
+            if q % 2 == 0:
+                h_planes[c, g] = new("h_planes", PACK * CH, BF16, bufs=3)
+            acc = bank(index)
+            for i in range(2):
+                matmul(acc[:, i * CH : (i + 1) * CH], w1_mx, (2 * q + i) * P, z_mx[c], 0, CH, True, True)
+            for i in range(2):
+                t = 2 * (q % 2) + i
+                nc.scalar.activation(
+                    out=h_planes[c, g][:, t * CH : (t + 1) * CH],
+                    in_=acc[:, i * CH : (i + 1) * CH],
+                    func=ACT.Relu,
+                    bias=b1_col[:, 2 * q + i : 2 * q + i + 1],
+                )
+
+        def interleave_h(c, g):
+            h_words[c, g] = new("h_words", PACK * CH, BF16, bufs=3)
+            nc.vector.tensor_copy(
+                out=h_words[c, g][:].rearrange("p (n i t) -> p n t i", i=4, t=PACK),
+                in_=h_planes[c, g][:].rearrange("p (t n i) -> p n t i", t=PACK, i=4),
+            )
+
+        def quantize_h(c, g):
+            h_mx[c, g] = (new("h_codes", CH, U32, bufs=4), new("h_scales", CH, U8, bufs=4))
+            quantize(h_mx[c, g][0], h_mx[c, g][1], h_words[c, g][:], 0, CH)
+
+        for r, (b0, b1e) in enumerate(PIECES):
+            full = min(b1e, L // GPB) - b0
+            blocks = d_bf[r][:].rearrange("p (k x) -> p k x", x=BANK)
+            nc.vector.memset(blocks[:, 0:full, PACK * A * GPB :], 0.0)
+        nc.vector.memset(d_bf[2][:, 2 * BANK + PACK * A * groups_in(N_BLK - 1) :], 0.0)
+
+        sigmoid(0)
+        nc.vector.tensor_copy(
+            out=d_spread[:].rearrange("p (n t) -> p n t", t=PACK),
+            in_=d_scale[:].unsqueeze(1).to_broadcast([P, GPB * A, PACK]),
+        )
+        gate_product(0)
+        acc0 = turn(gated[0], 0)
+        sigmoid(1)
+        widen(0, 0, 4)
+        turned_out(acc0, ws_t[0][:, 0:1024])
+        gate_product(1)
+        acc1 = turn(gated[1], 1)
+        sigmoid(2)
+        turned_out(acc1, ws_t[0][:, 1024:2048])
+        sigmoid(3)
+        quantize_dict(0)
+        widen(1, 4, 6)
+        quantize(ws_mx[0], ws_mx[1], ws_t[0][:], 0, 512)
+        widen(1, 6, 8)
+        gate_product(2)
+        quantize_dict(1)
+        for blk in range(0, 4):
+            expand(0, blk, 2 + blk)
+        acc2 = turn(gated[2], 6)
+        turned_out(acc2, ws_t[1][:, 0:1024])
+        widen(2, 8, 11)
+        gate_product(3)
+        quantize_dict(2)
+        for blk in range(4, 8):
+            expand(0, blk, (3 + blk) % 8)
+        acc3 = turn(gated[3], 3)
+        turned_out(acc3, ws_t[1][:, 1024:2048])
+        interleave_w1(0)
+        quantize(ws_mx[0], ws_mx[1], ws_t[1][:], 512, 512)
+        interleave_w1(1)
+        for blk in range(8, N_BLK):
+            expand(0, blk, blk - 4)
+        turn_z(0, 7)
+        quantize(w1_mx[0], w1_mx[1], w1_t[:], 0, H)
+        quantize_z(0)
+        for blk in range(0, 4):
+            expand(1, blk, blk)
+        quantize(weff_mx[0][0], weff_mx[0][1], weff[0][:, 0:4096], 0, 1024)
+        quantize(weff_mx[0][0], weff_mx[0][1], weff[0][:, 4096:5120], 1024, 256)
+        for q in range(4):
+            hidden(0, q, 4 + q)
+        interleave_h(0, 0)
+        interleave_h(0, 1)
+        quantize_h(0, 0)
+        quantize_h(0, 1)
+        for blk in range(4, N_BLK):
+            expand(1, blk, blk - 4)
+        turn_z(1, 7)
+        for k in range(XB):
+            quantize(weff_mx[1][0], weff_mx[1][1], weff[1][:, k * 1024 : (k + 1) * 1024], k * 256, 256)
+        quantize_z(1)
+
+        logits = {}
+        run_max = {}
+        top = {}
+        shifted = {}
+        expd = {}
+        sums = {}
+        small = {}
+        turned = {}
+        staged = {}
+
+        def logits_bank(c, k):
+            logits[c, k] = bank(k)
+            for i in range(2):
+                for g in range(2):
+                    matmul(
+                        logits[c, k][:, i * CH : (i + 1) * CH], weff_mx[g], (2 * k + i) * P, h_mx[c, g], 0, CH,
+                        g == 0, g == 1,
+                    )
+
+        def x_of(c, j):
+            return logits[c, j // 2][:, (j % 2) * CH : (j % 2 + 1) * CH]
+
+        def bias_of(j):
+            return b_col[:, 2 * j : 2 * j + 1]
+
+        def max_start(c):
+            for j in range(2):
+                run_max[c, j] = new("run_max%d" % j, CH, F32, bufs=2)
+                nc.scalar.activation(out=run_max[c, j][:], in_=x_of(c, j), func=ACT.Identity, bias=bias_of(j))
+
+        def max_step(c, j):
+            chain = run_max[c, j % 2]
+            nc.vector.scalar_tensor_tensor(
+                out=chain[:], in0=x_of(c, j), scalar=bias_of(j), in1=chain[:], op0=ALU.add, op1=ALU.max
+            )
+
+        def max_join(c):
+            small[c, "joined"] = new("joined", CH, F32, bufs=2)
+            nc.vector.tensor_tensor(
+                out=small[c, "joined"][:], in0=run_max[c, 0][:], in1=run_max[c, 1][:], op=ALU.max
+            )
+
+        def max_swap(c):
+            small[c, "swapped"] = new("swapped", CH, F32, bufs=2)
+            nc.scalar.copy(out=small[c, "swapped"][0:L, :], in_=small[c, "joined"][L:P, :])
+            nc.scalar.copy(out=small[c, "swapped"][L:P, :], in_=small[c, "joined"][0:L, :])
+
+        def max_cross(c):
+            top[c] = new("top", CH, F32, bufs=2)
+            nc.vector.tensor_tensor(out=top[c][:], in0=small[c, "joined"][:], in1=small[c, "swapped"][:], op=ALU.max)
+            shifted[c] = new("shifted", PAIRS * CH, F32, bufs=2)
+            expd[c] = new("expd", PAIRS * CH, F32, bufs=2)
+
+        def shift(c, j):
+            nc.vector.scalar_tensor_tensor(
+                out=shifted[c][:, j * CH : (j + 1) * CH], in0=x_of(c, j), scalar=bias_of(j), in1=top[c][:],
+                op0=ALU.add, op1=ALU.subtract,
+            )
+
+        def exponent(c, k):
+            cols = slice(k * BANK, (k + 1) * BANK)
+            nc.scalar.activation(out=expd[c][:, cols], in_=shifted[c][:, cols], func=ACT.Exp)
+
+        def sum_letters(c, i, acc):
+            for j in range(PAIRS):
+                nc.tensor.matmul(
+                    acc, lhsT=expd[c][:, j * CH + i * P : j * CH + (i + 1) * P],
+                    rhs=ident[:], start=(j == 0), stop=(j == PAIRS - 1), is_transpose=True,
+                )
+            sums[c, i] = acc
+
+        def sum_halves(c, i):
+            if i == 0:
+                small[c, "total"] = new("total", P, F32, bufs=2)
+            nc.vector.tensor_reduce(
+                out=small[c, "total"][:, i * L : (i + 1) * L],
+                in_=sums[c, i].rearrange("p (h g) -> p g h", h=2),
+                axis=AXIS.X,
+                op=ALU.add,
+            )
+
+        def logarithm(c):
+            small[c, "lse"] = new("lse", P, F32, bufs=2)
+            nc.scalar.activation(out=small[c, "lse"][:], in_=small[c, "total"][:], func=ACT.Ln)
+
+        def pairs_of(part):
+            return range(4 * part, min(4 * part + 4, PAIRS))
+
+        def turn_back(c, i, part, acc):
+            turned[c, i, part] = acc
+            for slot, j in enumerate(pairs_of(part)):
+                nc.tensor.transpose(
+                    acc[:, slot * P : (slot + 1) * P],
+                    shifted[c][:, j * CH + i * P : j * CH + (i + 1) * P], ident[:],
+                )
+
+        def finish(c, i, part):
+            if part == 0:
+                staged[c, i] = new("staged", O, F32, bufs=4)
+            letters = 2 * len(pairs_of(part))
+            nc.vector.tensor_tensor(
+                out=staged[c, i][:].rearrange("p (g a) -> p g a", a=A)[:, :, 8 * part : 8 * part + letters],
+                in0=turned[c, i, part].rearrange("p (a g) -> p g a", g=L),
+                in1=small[c, "lse"][:, i * L : (i + 1) * L].unsqueeze(2).to_broadcast([P, L, letters]),
+                op=ALU.subtract,
+            )
+            if part == 2:
+                nc.sync.dma_start(out=out_rows[c, i], in_=staged[c, i][:])
+
+        last = N_CH - 1
+        for k in range(XB):
+            logits_bank(0, k)
+        max_start(0)
+        for c in range(N_CH):
+            ahead = c < last
+            behind = c > 0
+            if ahead:
+                for q in range(4):
+                    hidden(c + 1, q, 5 + q % 3)
+            for j in range(2, PAIRS):
+                max_step(c, j)
+            if ahead:
+                interleave_h(c + 1, 0)
+            max_join(c)
+            max_swap(c)
+            if ahead:
+                quantize_h(c + 1, 0)
+                interleave_h(c + 1, 1)
+            max_cross(c)
+            if ahead:
+                quantize_h(c + 1, 1)
+            if behind:
+                for n, (i, part) in enumerate(((0, 0), (0, 1), (1, 0))):
+                    acc = bank((6, 7, 5)[n])
+                    turn_back(c - 1, i, part, acc[:])
+            for k in range(XB):
+                shift(c, 2 * k)
+                shift(c, 2 * k + 1)
+                exponent(c, k)
+                if ahead:
+                    logits_bank(c + 1, k)
+                elif k % 2 == 1:
+                    for i in range(2):
+                        acc = bank(k - 1 + i)
+                        turn_back(c, i, k // 2, acc[:])
+            if ahead:
+                max_start(c + 1)
+            if behind:
+                finish(c - 1, 0, 0)
+                acc = bank(6)
+                turn_back(c - 1, 1, 1, acc[:])
+                finish(c - 1, 0, 1)
+                acc = bank(7)
+                turn_back(c - 1, 0, 2, acc[:, 0:CH])
+                sum_letters(c, 0, acc[:, CH : CH + P])
+                finish(c - 1, 1, 0)
+                acc = bank(5)
+                turn_back(c - 1, 1, 2, acc[:, 0:CH])
+                sum_letters(c, 1, acc[:, CH : CH + P])
+                finish(c - 1, 1, 1)
+                sum_halves(c, 0)
+                finish(c - 1, 0, 2)
+                sum_halves(c, 1)
+                finish(c - 1, 1, 2)
+            else:
+                turn_z(2, 6)
+                turn_z(3, 7)
+                acc = bank(5)
+                for i in range(2):
+                    sum_letters(c, i, acc[:, i * P : (i + 1) * P])
+                quantize_z(2)
+                quantize_z(3)
+                for i in range(2):
+                    sum_halves(c, i)
+            logarithm(c)
+
+        acc = bank(XB - 1)
+        for i in range(2):
+            turn_back(last, i, 2, acc[:, i * CH : (i + 1) * CH])
+        for i in range(2):
+            for part in range(3):
+                finish(last, i, part)

@@ -91,27 +91,23 @@ def tile_gateddictionaryproteinprofiledecoder_kernel(tc, z, w1, b1, w, s, dict_b
             c0, c1 = piece_cols[r]
             nc.sync.dma_start(out=d_raw[r][:].rearrange("p (t n) -> p t n", t=PACK), in_=d_rows[:, :, c0:c1])
 
-        load_gate(0)
         nc.sync.dma_start(out=d_scale[:], in_=dict_scale.rearrange("(p t) o -> p (t o)", t=PACK))
-        load_w(0)
         load_dict(0)
-        load_gate(1)
-        load_w(1)
+        for q in range(4):
+            load_gate(q)
+            load_w(q)
         load_dict(1)
-        load_gate(2)
-        load_w(2)
         load_dict(2)
-        load_gate(3)
-        load_w(3)
         nc.sync.dma_start(out=w1_raw[:], in_=w1.rearrange("(p j) c -> p (j c)", j=PACK))
         nc.sync.dma_start(out=z_raw[0][:], in_=z_rows[0])
+        nc.sync.dma_start(out=z_raw[1][:], in_=z_rows[1])
         nc.sync.dma_start(
             out=b1_col[:].rearrange("p (g t) -> p g t", t=PACK), in_=b1.rearrange("(g p t) -> p g t", p=P, t=PACK)
         )
         b_rows = b.rearrange("(g a) -> g a", a=A)
         nc.sync.dma_start(out=b_col[0:L, :], in_=b_rows)
         nc.sync.dma_start(out=b_col[L:P, 0 : A - 1], in_=b_rows[:, 1:A])
-        for c in range(1, N_CH):
+        for c in range(2, N_CH):
             nc.sync.dma_start(out=z_raw[c][:], in_=z_rows[c])
 
         d_bf = [new("d_bf%d" % r, (b1e - b0) * BANK, BF16) for r, (b0, b1e) in enumerate(PIECES)]
@@ -120,7 +116,7 @@ def tile_gateddictionaryproteinprofiledecoder_kernel(tc, z, w1, b1, w, s, dict_b
         ws_mx = (new("ws_codes", H, U32), new("ws_scales", H, U8))
         w1_t = new("w1_t", PACK * H, BF16)
         w1_mx = (new("w1_codes", H, U32), new("w1_scales", H, U8))
-        weff = [new("weff%d" % g, PACK * O, BF16) for g in range(2)]
+        weff = [new("wide", PACK * O, BF16, bufs=2) for g in range(2)]
         weff_mx = [(new("weff_codes%d" % g, O, U32), new("weff_scales%d" % g, O, U8)) for g in range(2)]
         z_mx = [(new("z_codes%d" % c, CH, U32), new("z_scales%d" % c, CH, U8)) for c in range(N_CH)]
         d_spread = new("d_spread", PACK * GPB * A, F32)
@@ -171,14 +167,14 @@ def tile_gateddictionaryproteinprofiledecoder_kernel(tc, z, w1, b1, w, s, dict_b
             b0, b1e = PIECES[r]
             quantize(d_mx[0], d_mx[1], d_bf[r][:], b0 * P, (b1e - b0) * P)
 
-        def expand(g, blk, index):
+        def expand(g, blk, index, move=nc.scalar.copy):
             acc = bank(index)
             for t in range(PACK):
                 matmul(acc[:, t * P : (t + 1) * P], ws_mx, (g * PACK + t) * P, d_mx, blk * P, P, True, True)
             ng = groups_in(blk)
             src = acc[:].rearrange("p (t n) -> p t n", t=PACK)[:, :, 0 : ng * A].rearrange("p t (g a) -> p a g t", a=A)
             dst = weff[g][:].rearrange("p (a g t) -> p a g t", a=A, t=PACK)[:, :, GPB * blk : GPB * blk + ng, :]
-            nc.scalar.copy(out=dst, in_=src)
+            move(out=dst, in_=src)
 
         def interleave_w1(g):
             nc.vector.tensor_copy(
@@ -192,7 +188,7 @@ def tile_gateddictionaryproteinprofiledecoder_kernel(tc, z, w1, b1, w, s, dict_b
 
         def turn_z(c, index):
             acc = turn(z_raw[c], index)
-            z_t[c] = new("z_t", 2 * Z, BF16, bufs=2)
+            z_t[c] = new("z_t", 2 * Z, BF16, bufs=3)
             turned_out(acc, z_t[c][:])
 
         def quantize_z(c):
@@ -205,7 +201,7 @@ def tile_gateddictionaryproteinprofiledecoder_kernel(tc, z, w1, b1, w, s, dict_b
         def hidden(c, q, index):
             g = q // 2
             if q % 2 == 0:
-                h_planes[c, g] = new("h_planes", PACK * CH, BF16, bufs=3)
+                h_planes[c, g] = new("h_planes", PACK * CH, BF16, bufs=4)
             acc = bank(index)
             for i in range(2):
                 matmul(acc[:, i * CH : (i + 1) * CH], w1_mx, (2 * q + i) * P, z_mx[c], 0, CH, True, True)
@@ -235,62 +231,71 @@ def tile_gateddictionaryproteinprofiledecoder_kernel(tc, z, w1, b1, w, s, dict_b
             nc.vector.memset(blocks[:, 0:full, PACK * A * GPB :], 0.0)
         nc.vector.memset(d_bf[2][:, 2 * BANK + PACK * A * groups_in(N_BLK - 1) :], 0.0)
 
-        sigmoid(0)
         nc.vector.tensor_copy(
             out=d_spread[:].rearrange("p (n t) -> p n t", t=PACK),
             in_=d_scale[:].unsqueeze(1).to_broadcast([P, GPB * A, PACK]),
         )
+        widen(0, 0, 3)
+        sigmoid(0)
         gate_product(0)
         acc0 = turn(gated[0], 0)
         sigmoid(1)
-        widen(0, 0, 4)
-        turned_out(acc0, ws_t[0][:, 0:1024])
+        sigmoid(2)
         gate_product(1)
         acc1 = turn(gated[1], 1)
-        sigmoid(2)
-        turned_out(acc1, ws_t[0][:, 1024:2048])
+        turned_out(acc0, ws_t[0][:, 0:1024])
         sigmoid(3)
-        quantize_dict(0)
-        widen(1, 4, 6)
-        quantize(ws_mx[0], ws_mx[1], ws_t[0][:], 0, 512)
-        widen(1, 6, 8)
+        widen(0, 3, 4)
         gate_product(2)
-        quantize_dict(1)
-        for blk in range(0, 4):
-            expand(0, blk, 2 + blk)
-        acc2 = turn(gated[2], 6)
-        turned_out(acc2, ws_t[1][:, 0:1024])
-        widen(2, 8, 11)
+        acc2 = turn(gated[2], 2)
+        turned_out(acc1, ws_t[0][:, 1024:2048])
+        quantize_dict(0)
+        quantize(ws_mx[0], ws_mx[1], ws_t[0][:], 0, 512)
         gate_product(3)
-        quantize_dict(2)
-        for blk in range(4, 8):
-            expand(0, blk, (3 + blk) % 8)
+        turned_out(acc2, ws_t[1][:, 0:1024])
+        for blk in range(0, 2):
+            expand(0, blk, 4 + blk)
         acc3 = turn(gated[3], 3)
         turned_out(acc3, ws_t[1][:, 1024:2048])
-        interleave_w1(0)
+        for blk in range(2, 4):
+            expand(0, blk, 4 + blk)
+        widen(1, 4, 8)
         quantize(ws_mx[0], ws_mx[1], ws_t[1][:], 512, 512)
-        interleave_w1(1)
-        for blk in range(8, N_BLK):
-            expand(0, blk, blk - 4)
-        turn_z(0, 7)
-        quantize(w1_mx[0], w1_mx[1], w1_t[:], 0, H)
-        quantize_z(0)
+        quantize_dict(1)
         for blk in range(0, 4):
             expand(1, blk, blk)
+        widen(2, 8, 11)
+        interleave_w1(0)
+        quantize_dict(2)
+        interleave_w1(1)
+        for blk in range(4, 8):
+            expand(0, blk, blk)
+        turn_z(0, 0)
+        turn_z(1, 1)
+        for blk in range(8, N_BLK):
+            expand(0, blk, blk - 6)
+        quantize_z(0)
+        quantize(w1_mx[0], w1_mx[1], w1_t[:], 0, H)
+        quantize_z(1)
+        for blk in range(4, 6):
+            expand(1, blk, blk + 1)
+        for q in range(4):
+            hidden(0, q, (7 + q) % 8)
         quantize(weff_mx[0][0], weff_mx[0][1], weff[0][:, 0:4096], 0, 1024)
         quantize(weff_mx[0][0], weff_mx[0][1], weff[0][:, 4096:5120], 1024, 256)
-        for q in range(4):
-            hidden(0, q, 4 + q)
+        expand(1, 6, 3, nc.vector.tensor_copy)
+        expand(1, 7, 4, nc.vector.tensor_copy)
         interleave_h(0, 0)
         interleave_h(0, 1)
         quantize_h(0, 0)
         quantize_h(0, 1)
-        for blk in range(4, N_BLK):
-            expand(1, blk, blk - 4)
-        turn_z(1, 7)
+        for blk in range(8, N_BLK):
+            expand(1, blk, blk - 3)
+        hidden(1, 0, 1)
+        hidden(1, 1, 2)
+        turn_z(2, 5)
         for k in range(XB):
             quantize(weff_mx[1][0], weff_mx[1][1], weff[1][:, k * 1024 : (k + 1) * 1024], k * 256, 256)
-        quantize_z(1)
 
         logits = {}
         run_max = {}
@@ -342,8 +347,8 @@ def tile_gateddictionaryproteinprofiledecoder_kernel(tc, z, w1, b1, w, s, dict_b
         def max_cross(c):
             top[c] = new("top", CH, F32, bufs=2)
             nc.vector.tensor_tensor(out=top[c][:], in0=small[c, "joined"][:], in1=small[c, "swapped"][:], op=ALU.max)
-            shifted[c] = new("shifted", PAIRS * CH, F32, bufs=2)
-            expd[c] = new("expd", PAIRS * CH, F32, bufs=2)
+            shifted[c] = new("shifted", PAIRS * CH, F32, bufs=3)
+            expd[c] = new("wide", PAIRS * CH, F32, bufs=2)
 
         def shift(c, j):
             nc.vector.scalar_tensor_tensor(
@@ -355,27 +360,32 @@ def tile_gateddictionaryproteinprofiledecoder_kernel(tc, z, w1, b1, w, s, dict_b
             cols = slice(k * BANK, (k + 1) * BANK)
             nc.scalar.activation(out=expd[c][:, cols], in_=shifted[c][:, cols], func=ACT.Exp)
 
-        def sum_letters(c, i, acc):
-            for j in range(PAIRS):
-                nc.tensor.matmul(
-                    acc, lhsT=expd[c][:, j * CH + i * P : j * CH + (i + 1) * P],
-                    rhs=ident[:], start=(j == 0), stop=(j == PAIRS - 1), is_transpose=True,
-                )
-            sums[c, i] = acc
+        def add_letters(c, i, j, acc):
+            nc.tensor.matmul(
+                acc, lhsT=expd[c][:, j * CH + i * P : j * CH + (i + 1) * P],
+                rhs=ident[:], start=(j == 0), stop=(j == PAIRS - 1), is_transpose=True,
+            )
 
-        def sum_halves(c, i):
+        def sum_letters(c, i, index):
             if i == 0:
-                small[c, "total"] = new("total", P, F32, bufs=2)
+                sums[c] = bank(index)
+            for j in range(PAIRS):
+                add_letters(c, i, j, sums[c][:, i * P : (i + 1) * P])
+
+        def sum_halves(c, total):
             nc.vector.tensor_reduce(
-                out=small[c, "total"][:, i * L : (i + 1) * L],
-                in_=sums[c, i].rearrange("p (h g) -> p g h", h=2),
+                out=total.rearrange("p (i g) -> p i g", i=2),
+                in_=sums[c][:, 0:CH].rearrange("p (i h g) -> p i g h", i=2, h=2),
                 axis=AXIS.X,
                 op=ALU.add,
             )
 
-        def logarithm(c):
-            small[c, "lse"] = new("lse", P, F32, bufs=2)
-            nc.scalar.activation(out=small[c, "lse"][:], in_=small[c, "total"][:], func=ACT.Ln)
+        def logarithm(c0, c1):
+            cols = slice(c0 * P, c1 * P)
+            nc.scalar.activation(out=lse[:, cols], in_=totals[:, cols], func=ACT.Ln)
+
+        totals = new("totals", N_CH * P, F32)
+        lse = new("lse", N_CH * P, F32)
 
         def pairs_of(part):
             return range(4 * part, min(4 * part + 4, PAIRS))
@@ -389,88 +399,154 @@ def tile_gateddictionaryproteinprofiledecoder_kernel(tc, z, w1, b1, w, s, dict_b
                 )
 
         def finish(c, i, part):
-            if part == 0:
+            if (c, i) not in staged:
                 staged[c, i] = new("staged", O, F32, bufs=4)
             letters = 2 * len(pairs_of(part))
             nc.vector.tensor_tensor(
                 out=staged[c, i][:].rearrange("p (g a) -> p g a", a=A)[:, :, 8 * part : 8 * part + letters],
                 in0=turned[c, i, part].rearrange("p (a g) -> p g a", g=L),
-                in1=small[c, "lse"][:, i * L : (i + 1) * L].unsqueeze(2).to_broadcast([P, L, letters]),
+                in1=lse[:, c * P + i * L : c * P + (i + 1) * L].unsqueeze(2).to_broadcast([P, L, letters]),
                 op=ALU.subtract,
             )
-            if part == 2:
-                nc.sync.dma_start(out=out_rows[c, i], in_=staged[c, i][:])
 
-        last = N_CH - 1
-        for k in range(XB):
-            logits_bank(0, k)
-        max_start(0)
-        for c in range(N_CH):
-            ahead = c < last
-            behind = c > 0
-            if ahead:
-                for q in range(4):
-                    hidden(c + 1, q, 5 + q % 3)
+        def store(c, i):
+            nc.sync.dma_start(out=out_rows[c, i], in_=staged[c, i][:])
+
+        def turn_part(c, i, part, index):
+            acc = bank(index)
+            turn_back(c, i, part, acc[:])
+
+        def turn_ends(c, index):
+            acc = bank(index)
+            for i in range(2):
+                turn_back(c, i, 2, acc[:, i * CH : (i + 1) * CH])
+
+        def reduce_sums(c):
+            sum_halves(c, totals[:, c * P : (c + 1) * P])
+
+        def max_with_hidden(c):
+            if c > 0:
+                hidden(c + 1, 2, 6)
+                hidden(c + 1, 3, 7)
+                sum_letters(c - 1, 0, 5)
+                sum_letters(c - 1, 1, 5)
             for j in range(2, PAIRS):
                 max_step(c, j)
-            if ahead:
-                interleave_h(c + 1, 0)
+            interleave_h(c + 1, 0)
             max_join(c)
             max_swap(c)
-            if ahead:
-                quantize_h(c + 1, 0)
-                interleave_h(c + 1, 1)
+            if c == 1:
+                hidden(3, 0, 6)
+                hidden(3, 1, 7)
+            quantize_h(c + 1, 0)
+            interleave_h(c + 1, 1)
+            if c > 0:
+                reduce_sums(c - 1)
             max_cross(c)
-            if ahead:
-                quantize_h(c + 1, 1)
-            if behind:
-                for n, (i, part) in enumerate(((0, 0), (0, 1), (1, 0))):
-                    acc = bank((6, 7, 5)[n])
-                    turn_back(c - 1, i, part, acc[:])
-            for k in range(XB):
-                shift(c, 2 * k)
-                shift(c, 2 * k + 1)
-                exponent(c, k)
-                if ahead:
-                    logits_bank(c + 1, k)
-                elif k % 2 == 1:
-                    for i in range(2):
-                        acc = bank(k - 1 + i)
-                        turn_back(c, i, k // 2, acc[:])
-            if ahead:
-                max_start(c + 1)
-            if behind:
-                finish(c - 1, 0, 0)
-                acc = bank(6)
-                turn_back(c - 1, 1, 1, acc[:])
-                finish(c - 1, 0, 1)
-                acc = bank(7)
-                turn_back(c - 1, 0, 2, acc[:, 0:CH])
-                sum_letters(c, 0, acc[:, CH : CH + P])
-                finish(c - 1, 1, 0)
-                acc = bank(5)
-                turn_back(c - 1, 1, 2, acc[:, 0:CH])
-                sum_letters(c, 1, acc[:, CH : CH + P])
-                finish(c - 1, 1, 1)
-                sum_halves(c, 0)
-                finish(c - 1, 0, 2)
-                sum_halves(c, 1)
-                finish(c - 1, 1, 2)
-            else:
-                turn_z(2, 6)
-                turn_z(3, 7)
-                acc = bank(5)
-                for i in range(2):
-                    sum_letters(c, i, acc[:, i * P : (i + 1) * P])
-                quantize_z(2)
-                quantize_z(3)
-                for i in range(2):
-                    sum_halves(c, i)
-            logarithm(c)
+            quantize_h(c + 1, 1)
 
-        acc = bank(XB - 1)
+        def shift_bank(c, k):
+            shift(c, 2 * k)
+            shift(c, 2 * k + 1)
+            exponent(c, k)
+
+        logits_bank(0, 0)
+        max_start(0)
+        logits_bank(0, 1)
+        hidden(1, 2, 6)
+        hidden(1, 3, 7)
+        quantize_z(2)
+        for k in range(2, XB):
+            logits_bank(0, k)
+        turn_z(3, 5)
+        hidden(2, 0, 6)
+        hidden(2, 1, 7)
+        max_with_hidden(0)
+        for c in range(2):
+            for k in range(XB):
+                shift_bank(c, k)
+                logits_bank(c + 1, k)
+                if k == 1:
+                    max_start(c + 1)
+            if c == 0:
+                quantize_z(3)
+            max_with_hidden(c + 1)
+        logarithm(0, 2)
+
+        turn_part(0, 0, 0, 6)
+        turn_part(0, 0, 1, 7)
+        turn_ends(0, 5)
+        for k in range(XB):
+            shift_bank(2, k)
+            logits_bank(3, k)
+        max_start(3)
+        finish(0, 0, 0)
+        turn_part(0, 1, 0, 6)
+        finish(0, 0, 1)
+        turn_part(0, 1, 1, 7)
+        finish(0, 0, 2)
+        store(0, 0)
+        finish(0, 1, 2)
+        turn_part(1, 0, 0, 5)
+        finish(0, 1, 0)
+        turn_part(1, 0, 1, 6)
+        finish(0, 1, 1)
+        store(0, 1)
+        turn_ends(1, 7)
+        finish(1, 0, 0)
+        turn_part(1, 1, 0, 5)
+        finish(1, 0, 1)
+        turn_part(1, 1, 1, 6)
+        finish(1, 0, 2)
+        store(1, 0)
+        finish(1, 1, 2)
+        sum_letters(2, 0, 7)
+        sum_letters(2, 1, 7)
+        finish(1, 1, 0)
+        finish(1, 1, 1)
+        store(1, 1)
+
+        turn_part(2, 0, 0, 5)
+        turn_part(2, 0, 1, 6)
+        for j in range(2, PAIRS):
+            max_step(3, j)
+            if j == PAIRS - 2:
+                reduce_sums(2)
+                logarithm(2, 3)
+        turn_ends(2, 7)
+        max_join(3)
+        max_swap(3)
+        finish(2, 0, 0)
+        finish(2, 0, 1)
+        max_cross(3)
+        finish(2, 0, 2)
+        store(2, 0)
+        turn_part(2, 1, 0, 5)
+        turn_part(2, 1, 1, 6)
+        for k in range(XB):
+            shift_bank(3, k)
+        turn_part(3, 0, 0, 0)
+        tail_sums = [bank(1 + i) for i in range(2)]
+        for j in range(PAIRS):
+            for i in range(2):
+                add_letters(3, i, j, tail_sums[i][:, 0:P])
+        turn_part(3, 0, 1, 3)
+        turn_ends(3, 4)
+        finish(2, 1, 2)
+        turn_part(3, 1, 0, 7)
+        finish(2, 1, 0)
+        turn_part(3, 1, 1, 5)
+        finish(2, 1, 1)
+        store(2, 1)
         for i in range(2):
-            turn_back(last, i, 2, acc[:, i * CH : (i + 1) * CH])
+            nc.vector.tensor_reduce(
+                out=totals[:, 3 * P + i * L : 3 * P + (i + 1) * L],
+                in_=tail_sums[i][:, 0:P].rearrange("p (h g) -> p g h", h=2),
+                axis=AXIS.X,
+                op=ALU.add,
+            )
+        logarithm(3, 4)
         for i in range(2):
             for part in range(3):
-                finish(last, i, part)
+                finish(3, i, part)
+            store(3, i)

@@ -36,8 +36,8 @@ def tile_gateddictionaryproteinprofiledecoder_kernel(tc, z, w1, b1, w, s, dict_b
         sb = ctx.enter_context(tc.tile_pool(name="sb", bufs=1))
         ps = ctx.enter_context(tc.psum_pool(name="ps", bufs=1))
 
-        def new(name, width, dtype, bufs=1):
-            return sb.tile([P, width], dtype, name=name, tag=name, bufs=bufs, align_bytes=64)
+        def new(name, width, dtype, bufs=1, tag=None):
+            return sb.tile([P, width], dtype, name=name, tag=tag or name, bufs=bufs, align_bytes=64)
 
         def bank(index):
             return ps.tile([P, BANK], F32, name="bank%d" % index, tag="bank%d" % index)
@@ -119,7 +119,6 @@ def tile_gateddictionaryproteinprofiledecoder_kernel(tc, z, w1, b1, w, s, dict_b
         weff = [new("wide", PACK * O, BF16, bufs=2) for g in range(2)]
         weff_mx = [(new("weff_codes%d" % g, O, U32), new("weff_scales%d" % g, O, U8)) for g in range(2)]
         z_mx = [(new("z_codes%d" % c, CH, U32), new("z_scales%d" % c, CH, U8)) for c in range(N_CH)]
-        d_spread = new("d_spread", PACK * GPB * A, F32)
         gate = {}
         gated = {}
 
@@ -149,19 +148,34 @@ def tile_gateddictionaryproteinprofiledecoder_kernel(tc, z, w1, b1, w, s, dict_b
                 in_=acc[:].rearrange("p (i u r) -> p i r u", i=2, u=2),
             )
 
-        def widen(r, blk0, blk1):
+        d_planes = {}
+
+        def widen(r, slots, on_scalar=False):
+            width = piece_cols[r][1] - piece_cols[r][0]
+            if r not in d_planes:
+                d_planes[r] = new("d_planes", PACK * width, BF16, bufs=2, tag="staged")
+            for t in slots:
+                cols = slice(t * width, (t + 1) * width)
+                codes = d_raw[r][:, cols].bitcast(FP8)
+                if on_scalar:
+                    nc.scalar.activation(
+                        out=d_planes[r][:, cols], in_=codes, func=ACT.Copy, scale=d_scale[:, t : t + 1]
+                    )
+                else:
+                    nc.vector.tensor_scalar(
+                        out=d_planes[r][:, cols], in0=codes, scalar1=d_scale[:, t : t + 1], scalar2=None, op0=ALU.mult
+                    )
+
+        def interleave_dict(r, blk0, blk1):
             first = PIECES[r][0]
-            codes = d_raw[r][:].bitcast(FP8).rearrange("p (t n) -> p n t", t=PACK)
-            for blk in range(blk0, blk1):
-                cols = A * groups_in(blk)
-                c0 = (blk - first) * GPB * A
-                x0 = (blk - first) * BANK
-                nc.vector.tensor_tensor(
-                    out=d_bf[r][:, x0 : x0 + PACK * cols].rearrange("p (n t) -> p n t", t=PACK),
-                    in0=codes[:, c0 : c0 + cols, :],
-                    in1=d_spread[:, 0 : PACK * cols].rearrange("p (n t) -> p n t", t=PACK),
-                    op=ALU.mult,
-                )
+            cols = A * groups_in(blk0)
+            c0 = (blk0 - first) * GPB * A
+            src = d_planes[r][:].rearrange("p (t n) -> p t n", t=PACK)[:, :, c0 : c0 + (blk1 - blk0) * cols]
+            dst = d_bf[r][:].rearrange("p (k x) -> p k x", x=BANK)[:, blk0 - first : blk1 - first, 0 : PACK * cols]
+            nc.vector.tensor_copy(
+                out=dst.rearrange("p k (n i t) -> p k n t i", i=4, t=PACK),
+                in_=src.rearrange("p t (k n i) -> p k n t i", k=blk1 - blk0, i=4),
+            )
 
         def quantize_dict(r):
             b0, b1e = PIECES[r]
@@ -198,28 +212,43 @@ def tile_gateddictionaryproteinprofiledecoder_kernel(tc, z, w1, b1, w, s, dict_b
         h_words = {}
         h_mx = {}
 
-        def hidden(c, q, index):
+        h_acc = {}
+
+        def hidden_matmul(c, q, index):
+            h_acc[c, q] = bank(index)
+            for i in range(2):
+                matmul(h_acc[c, q][:, i * CH : (i + 1) * CH], w1_mx, (2 * q + i) * P, z_mx[c], 0, CH, True, True)
+
+        def hidden_out(c, q):
             g = q // 2
             if q % 2 == 0:
                 h_planes[c, g] = new("h_planes", PACK * CH, BF16, bufs=4)
-            acc = bank(index)
-            for i in range(2):
-                matmul(acc[:, i * CH : (i + 1) * CH], w1_mx, (2 * q + i) * P, z_mx[c], 0, CH, True, True)
             for i in range(2):
                 t = 2 * (q % 2) + i
                 nc.scalar.activation(
                     out=h_planes[c, g][:, t * CH : (t + 1) * CH],
-                    in_=acc[:, i * CH : (i + 1) * CH],
+                    in_=h_acc[c, q][:, i * CH : (i + 1) * CH],
                     func=ACT.Relu,
                     bias=b1_col[:, 2 * q + i : 2 * q + i + 1],
                 )
 
-        def interleave_h(c, g):
-            h_words[c, g] = new("h_words", PACK * CH, BF16, bufs=3)
-            nc.vector.tensor_copy(
-                out=h_words[c, g][:].rearrange("p (n i t) -> p n t i", i=4, t=PACK),
-                in_=h_planes[c, g][:].rearrange("p (t n i) -> p n t i", t=PACK, i=4),
-            )
+        def hidden(c, q, index):
+            hidden_matmul(c, q, index)
+            hidden_out(c, q)
+
+        def interleave_h(c, g, on_gpsimd=False):
+            h_words[c, g] = new("h_words%d" % g, PACK * CH, BF16)
+            if on_gpsimd:
+                nc.gpsimd.tensor_scalar(
+                    out=h_words[c, g][:].rearrange("p (n t) -> p n t", t=PACK),
+                    in0=h_planes[c, g][:].rearrange("p (t n) -> p n t", t=PACK),
+                    scalar1=1.0, scalar2=0.0, op0=ALU.mult, op1=ALU.add,
+                )
+            else:
+                nc.vector.tensor_copy(
+                    out=h_words[c, g][:].rearrange("p (n i t) -> p n t i", i=4, t=PACK),
+                    in_=h_planes[c, g][:].rearrange("p (t n i) -> p n t i", t=PACK, i=4),
+                )
 
         def quantize_h(c, g):
             h_mx[c, g] = (new("h_codes", CH, U32, bufs=4), new("h_scales", CH, U8, bufs=4))
@@ -231,69 +260,73 @@ def tile_gateddictionaryproteinprofiledecoder_kernel(tc, z, w1, b1, w, s, dict_b
             nc.vector.memset(blocks[:, 0:full, PACK * A * GPB :], 0.0)
         nc.vector.memset(d_bf[2][:, 2 * BANK + PACK * A * groups_in(N_BLK - 1) :], 0.0)
 
-        nc.vector.tensor_copy(
-            out=d_spread[:].rearrange("p (n t) -> p n t", t=PACK),
-            in_=d_scale[:].unsqueeze(1).to_broadcast([P, GPB * A, PACK]),
-        )
-        widen(0, 0, 3)
+        widen(0, range(PACK))
         sigmoid(0)
+        interleave_dict(0, 0, 2)
         gate_product(0)
         acc0 = turn(gated[0], 0)
         sigmoid(1)
         sigmoid(2)
+        interleave_dict(0, 2, 4)
         gate_product(1)
         acc1 = turn(gated[1], 1)
         turned_out(acc0, ws_t[0][:, 0:1024])
         sigmoid(3)
-        widen(0, 3, 4)
+        quantize_dict(0)
         gate_product(2)
         acc2 = turn(gated[2], 2)
         turned_out(acc1, ws_t[0][:, 1024:2048])
-        quantize_dict(0)
+        widen(1, range(0, 2), True)
+        widen(2, range(PACK))
         quantize(ws_mx[0], ws_mx[1], ws_t[0][:], 0, 512)
         gate_product(3)
         turned_out(acc2, ws_t[1][:, 0:1024])
+        widen(1, range(2, PACK), True)
         for blk in range(0, 2):
             expand(0, blk, 4 + blk)
         acc3 = turn(gated[3], 3)
         turned_out(acc3, ws_t[1][:, 1024:2048])
         for blk in range(2, 4):
             expand(0, blk, 4 + blk)
-        widen(1, 4, 8)
-        quantize(ws_mx[0], ws_mx[1], ws_t[1][:], 512, 512)
-        quantize_dict(1)
-        for blk in range(0, 4):
-            expand(1, blk, blk)
-        widen(2, 8, 11)
-        interleave_w1(0)
+        interleave_dict(2, 8, 10)
+        interleave_dict(2, 10, 11)
+        interleave_dict(1, 4, 8)
         quantize_dict(2)
-        interleave_w1(1)
-        for blk in range(4, 8):
-            expand(0, blk, blk)
-        turn_z(0, 0)
-        turn_z(1, 1)
+        quantize_dict(1)
+        quantize(ws_mx[0], ws_mx[1], ws_t[1][:], 512, 512)
         for blk in range(8, N_BLK):
-            expand(0, blk, blk - 6)
-        quantize_z(0)
-        quantize(w1_mx[0], w1_mx[1], w1_t[:], 0, H)
-        quantize_z(1)
+            expand(0, blk, blk - 8)
+        interleave_w1(0)
+        interleave_w1(1)
         for blk in range(4, 6):
-            expand(1, blk, blk + 1)
+            expand(0, blk, blk - 1)
+        for blk in range(0, 1):
+            expand(1, blk, 5 + blk, nc.vector.tensor_copy)
+        for blk in range(6, 8):
+            expand(0, blk, blk - 6)
+        turn_z(0, 2)
+        turn_z(1, 3)
+        quantize(w1_mx[0], w1_mx[1], w1_t[:], 0, H)
+        quantize_z(0)
+        quantize_z(1)
+        for blk in range(1, 4):
+            expand(1, blk, blk + 4)
         for q in range(4):
-            hidden(0, q, (7 + q) % 8)
+            hidden(0, q, q)
         quantize(weff_mx[0][0], weff_mx[0][1], weff[0][:, 0:4096], 0, 1024)
         quantize(weff_mx[0][0], weff_mx[0][1], weff[0][:, 4096:5120], 1024, 256)
-        expand(1, 6, 3, nc.vector.tensor_copy)
-        expand(1, 7, 4, nc.vector.tensor_copy)
+        for blk in range(4, 7):
+            expand(1, blk, blk, nc.vector.tensor_copy)
         interleave_h(0, 0)
         interleave_h(0, 1)
         quantize_h(0, 0)
         quantize_h(0, 1)
-        for blk in range(8, N_BLK):
-            expand(1, blk, blk - 3)
-        hidden(1, 0, 1)
-        hidden(1, 1, 2)
+        for blk in range(7, N_BLK):
+            expand(1, blk, blk % 8)
+        hidden(1, 0, 3)
+        hidden(1, 1, 4)
         turn_z(2, 5)
+        z3_acc = turn(z_raw[3], 7)
         for k in range(XB):
             quantize(weff_mx[1][0], weff_mx[1][1], weff[1][:, k * 1024 : (k + 1) * 1024], k * 256, 256)
 
@@ -398,19 +431,33 @@ def tile_gateddictionaryproteinprofiledecoder_kernel(tc, z, w1, b1, w, s, dict_b
                     shifted[c][:, j * CH + i * P : j * CH + (i + 1) * P], ident[:],
                 )
 
-        def finish(c, i, part):
-            if (c, i) not in staged:
-                staged[c, i] = new("staged", O, F32, bufs=4)
+        def staged_of(c):
+            if c not in staged:
+                staged[c] = new("staged", 2 * O, F32, bufs=2)
+            return staged[c][:].rearrange("p (i g a) -> p i g a", i=2, a=A)
+
+        def finish(c, i, part, groups=slice(0, L)):
             letters = 2 * len(pairs_of(part))
+            count = groups.stop - groups.start
+            first = c * P + i * L
             nc.vector.tensor_tensor(
-                out=staged[c, i][:].rearrange("p (g a) -> p g a", a=A)[:, :, 8 * part : 8 * part + letters],
-                in0=turned[c, i, part].rearrange("p (a g) -> p g a", g=L),
-                in1=lse[:, c * P + i * L : c * P + (i + 1) * L].unsqueeze(2).to_broadcast([P, L, letters]),
+                out=staged_of(c)[:, i, groups, 8 * part : 8 * part + letters],
+                in0=turned[c, i, part].rearrange("p (a g) -> p g a", g=L)[:, groups, :],
+                in1=lse[:, first + groups.start : first + groups.stop].unsqueeze(2).to_broadcast([P, count, letters]),
                 op=ALU.subtract,
             )
 
-        def store(c, i):
-            nc.sync.dma_start(out=out_rows[c, i], in_=staged[c, i][:])
+        def finish_ends(c):
+            nc.vector.tensor_tensor(
+                out=staged_of(c)[:, :, :, 16:A],
+                in0=turned[c, "ends"].rearrange("p (i a g) -> p i g a", i=2, g=L),
+                in1=lse[:, c * P : (c + 1) * P].rearrange("p (i g) -> p i g", i=2).unsqueeze(3).to_broadcast([P, 2, L, 4]),
+                op=ALU.subtract,
+            )
+
+        def store(c, i, groups=slice(0, L)):
+            cols = slice(groups.start * A, groups.stop * A)
+            nc.sync.dma_start(out=out_rows[c, i][:, cols], in_=staged[c][:, i * O + cols.start : i * O + cols.stop])
 
         def turn_part(c, i, part, index):
             acc = bank(index)
@@ -418,110 +465,137 @@ def tile_gateddictionaryproteinprofiledecoder_kernel(tc, z, w1, b1, w, s, dict_b
 
         def turn_ends(c, index):
             acc = bank(index)
+            turned[c, "ends"] = acc[:]
             for i in range(2):
                 turn_back(c, i, 2, acc[:, i * CH : (i + 1) * CH])
 
         def reduce_sums(c):
             sum_halves(c, totals[:, c * P : (c + 1) * P])
 
-        def max_with_hidden(c):
-            if c > 0:
-                hidden(c + 1, 2, 6)
-                hidden(c + 1, 3, 7)
-                sum_letters(c - 1, 0, 5)
-                sum_letters(c - 1, 1, 5)
-            for j in range(2, PAIRS):
-                max_step(c, j)
-            interleave_h(c + 1, 0)
-            max_join(c)
-            max_swap(c)
-            if c == 1:
-                hidden(3, 0, 6)
-                hidden(3, 1, 7)
-            quantize_h(c + 1, 0)
-            interleave_h(c + 1, 1)
-            if c > 0:
-                reduce_sums(c - 1)
-            max_cross(c)
-            quantize_h(c + 1, 1)
-
         def shift_bank(c, k):
             shift(c, 2 * k)
             shift(c, 2 * k + 1)
             exponent(c, k)
 
+        def max_steps(c):
+            for j in range(2, PAIRS):
+                max_step(c, j)
+
         logits_bank(0, 0)
         max_start(0)
         logits_bank(0, 1)
         hidden(1, 2, 6)
-        hidden(1, 3, 7)
+        hidden(1, 3, 5)
         quantize_z(2)
+        z_t[3] = new("z_t", 2 * Z, BF16, bufs=3)
+        turned_out(z3_acc, z_t[3][:])
         for k in range(2, XB):
             logits_bank(0, k)
-        turn_z(3, 5)
         hidden(2, 0, 6)
-        hidden(2, 1, 7)
-        max_with_hidden(0)
-        for c in range(2):
-            for k in range(XB):
-                shift_bank(c, k)
-                logits_bank(c + 1, k)
-                if k == 1:
-                    max_start(c + 1)
-            if c == 0:
-                quantize_z(3)
-            max_with_hidden(c + 1)
-        logarithm(0, 2)
+        hidden(2, 1, 5)
+        hidden_matmul(2, 2, 7)
+        hidden_matmul(2, 3, 6)
+        max_steps(0)
+        interleave_h(1, 0)
+        max_join(0)
+        max_swap(0)
+        interleave_h(1, 1)
+        quantize_z(3)
+        quantize_h(1, 1)
+        max_cross(0)
+        quantize_h(1, 0)
+        interleave_h(2, 0, True)
+        for k in range(XB):
+            shift_bank(0, k)
+            logits_bank(1, k)
+            if k == 1:
+                max_start(1)
 
-        turn_part(0, 0, 0, 6)
+        hidden_out(2, 2)
+        hidden_out(2, 3)
+        sum_letters(0, 0, 5)
+        sum_letters(0, 1, 5)
+        hidden_matmul(3, 0, 7)
+        hidden_matmul(3, 1, 6)
+        max_steps(1)
+        quantize_h(2, 0)
+        max_join(1)
+        max_swap(1)
+        hidden_out(3, 0)
+        hidden_out(3, 1)
+        interleave_h(3, 0, True)
+        interleave_h(2, 1)
+        reduce_sums(0)
+        max_cross(1)
+        quantize_h(2, 1)
+        hidden_matmul(3, 2, 5)
+        hidden_matmul(3, 3, 7)
+        for k in range(XB):
+            shift_bank(1, k)
+            logits_bank(2, k)
+            if k == 1:
+                max_start(2)
+
+        hidden_out(3, 2)
+        hidden_out(3, 3)
+        sum_letters(1, 0, 6)
+        sum_letters(1, 1, 6)
+        max_steps(2)
+        quantize_h(3, 0)
+        max_join(2)
+        max_swap(2)
+        interleave_h(3, 1)
+        reduce_sums(1)
+        logarithm(0, 2)
+        max_cross(2)
+        quantize_h(3, 1)
+
+        turn_part(0, 0, 0, 5)
         turn_part(0, 0, 1, 7)
-        turn_ends(0, 5)
+        turn_ends(0, 6)
         for k in range(XB):
             shift_bank(2, k)
-            logits_bank(3, k)
+            if k < 4:
+                logits_bank(3, k)
+        turn_part(0, 1, 0, 4)
         max_start(3)
         finish(0, 0, 0)
-        turn_part(0, 1, 0, 6)
+        turn_part(0, 1, 1, 5)
         finish(0, 0, 1)
-        turn_part(0, 1, 1, 7)
-        finish(0, 0, 2)
+        turn_part(1, 0, 0, 7)
+        finish_ends(0)
         store(0, 0)
-        finish(0, 1, 2)
-        turn_part(1, 0, 0, 5)
+        turn_ends(1, 6)
         finish(0, 1, 0)
-        turn_part(1, 0, 1, 6)
+        logits_bank(3, 4)
         finish(0, 1, 1)
         store(0, 1)
-        turn_ends(1, 7)
+        turn_part(1, 0, 1, 5)
         finish(1, 0, 0)
-        turn_part(1, 1, 0, 5)
-        finish(1, 0, 1)
+        turn_part(1, 1, 0, 7)
+        finish_ends(1)
         turn_part(1, 1, 1, 6)
-        finish(1, 0, 2)
+        finish(1, 0, 1)
         store(1, 0)
-        finish(1, 1, 2)
-        sum_letters(2, 0, 7)
-        sum_letters(2, 1, 7)
+        sum_letters(2, 0, 5)
+        sum_letters(2, 1, 5)
         finish(1, 1, 0)
+        turn_part(2, 0, 0, 7)
         finish(1, 1, 1)
         store(1, 1)
-
-        turn_part(2, 0, 0, 5)
         turn_part(2, 0, 1, 6)
+
         for j in range(2, PAIRS):
             max_step(3, j)
-            if j == PAIRS - 2:
-                reduce_sums(2)
-                logarithm(2, 3)
-        turn_ends(2, 7)
+        reduce_sums(2)
+        logarithm(2, 3)
+        turn_ends(2, 5)
         max_join(3)
         max_swap(3)
         finish(2, 0, 0)
         finish(2, 0, 1)
         max_cross(3)
-        finish(2, 0, 2)
-        store(2, 0)
-        turn_part(2, 1, 0, 5)
+        turn_part(2, 1, 0, 7)
         turn_part(2, 1, 1, 6)
         for k in range(XB):
             shift_bank(3, k)
@@ -532,10 +606,11 @@ def tile_gateddictionaryproteinprofiledecoder_kernel(tc, z, w1, b1, w, s, dict_b
                 add_letters(3, i, j, tail_sums[i][:, 0:P])
         turn_part(3, 0, 1, 3)
         turn_ends(3, 4)
-        finish(2, 1, 2)
-        turn_part(3, 1, 0, 7)
+        finish_ends(2)
+        store(2, 0)
+        turn_part(3, 1, 0, 5)
         finish(2, 1, 0)
-        turn_part(3, 1, 1, 5)
+        turn_part(3, 1, 1, 7)
         finish(2, 1, 1)
         store(2, 1)
         for i in range(2):
@@ -547,6 +622,7 @@ def tile_gateddictionaryproteinprofiledecoder_kernel(tc, z, w1, b1, w, s, dict_b
             )
         logarithm(3, 4)
         for i in range(2):
-            for part in range(3):
-                finish(3, i, part)
-            store(3, i)
+            for groups in (slice(0, L // 2), slice(L // 2, L)):
+                for part in range(3):
+                    finish(3, i, part, groups)
+                store(3, i, groups)

from contextlib import ExitStack

import concourse.mybir as mybir
from concourse.masks import make_identity

B, Z, H, C, L, A = 1024, 512, 1024, 512, 64, 20
O = L * A
FLOPS = 2 * (B * Z * H + H * C * O + B * H * O)

F32 = mybir.dt.float32
BF16 = mybir.dt.bfloat16
U32 = mybir.dt.uint32
U8 = mybir.dt.uint8
FP8 = mybir.dt.float8_e4m3fn
FP8X4 = mybir.dt.float8_e4m3fn_x4
ALU = mybir.AluOpType
ACT = mybir.ActivationFunctionType
AXIS = mybir.AxisListType

P = 128
PACK = 4
BANK = 512
CH = 256
N_CH = B // CH
PAIRS = A // 2
XB = PAIRS // 2
GPB = 6
N_BLK = (L + GPB - 1) // GPB
PIECES = ((0, 4), (4, 8), (8, 11))


def tile_gateddictionaryproteinprofiledecoder_kernel(tc, z, w1, b1, w, s, dict_bytes, dict_scale, b, out):
    nc = tc.nc

    with ExitStack() as ctx:
        sb = ctx.enter_context(tc.tile_pool(name="sb", bufs=1))
        ps = ctx.enter_context(tc.psum_pool(name="ps", bufs=1))

        def new(name, width, dtype, bufs=1, tag=None):
            return sb.tile([P, width], dtype, name=name, tag=tag or name, bufs=bufs, align_bytes=64)

        def bank(index):
            return ps.tile([P, BANK], F32, name="bank%d" % index, tag="bank%d" % index)

        def quantize(codes, scales, values, first, count):
            nc.vector.quantize_mx(
                out=codes[:, first : first + count].bitcast(FP8X4),
                scales=scales[:, first : first + count],
                in_=values,
            )

        def matmul(acc, lhs, lhs_first, rhs, rhs_first, count, start, stop):
            nc.tensor.matmul_mx(
                out=acc,
                lhsT=lhs[0][:, lhs_first : lhs_first + P].bitcast(FP8X4),
                lhsT_scale=lhs[1][:, lhs_first : lhs_first + P],
                rhs=rhs[0][:, rhs_first : rhs_first + count].bitcast(FP8X4),
                rhs_scale=rhs[1][:, rhs_first : rhs_first + count],
                start=start,
                stop=stop,
            )

        ident = new("ident", P, F32)
        make_identity(nc, ident[:])

        ctx.enter_context(tc.manual_schedule())

        s_rows = s.rearrange("(g m u i) k -> g u m (i k)", g=2, u=2, i=2)
        w_rows = w.rearrange("(g m u i) k -> g u m (i k)", g=2, u=2, i=2)
        d_rows = dict_bytes.rearrange("(p t) n -> p t n", t=PACK)
        z_rows = z.rearrange("(c p i) k -> c p (i k)", p=P, i=2)
        out_rows = out.rearrange("(c p i) l a -> c i p (l a)", p=P, i=2)

        s_raw = [new("s_raw%d" % q, 2 * C, BF16) for q in range(4)]
        w_raw = [new("w_raw%d" % q, 2 * C, BF16) for q in range(4)]
        piece_cols = [(GPB * A * b0, min(GPB * A * b1e, O)) for b0, b1e in PIECES]
        d_raw = [new("dict_raw%d" % r, PACK * (c1 - c0), U8) for r, (c0, c1) in enumerate(piece_cols)]
        d_scale = new("d_scale", PACK, F32)
        w1_raw = new("w1_raw", PACK * H, BF16)
        z_raw = [new("z_raw%d" % c, 2 * Z, BF16) for c in range(N_CH)]
        b1_col = new("b1_col", 8, BF16)
        b_col = new("b_col", A, BF16)

        def load_gate(q):
            nc.sync.dma_start(out=s_raw[q][:], in_=s_rows[q // 2, q % 2])

        def load_w(q):
            nc.sync.dma_start(out=w_raw[q][:], in_=w_rows[q // 2, q % 2])

        def load_dict(r):
            c0, c1 = piece_cols[r]
            nc.sync.dma_start(out=d_raw[r][:].rearrange("p (t n) -> p t n", t=PACK), in_=d_rows[:, :, c0:c1])

        nc.sync.dma_start(out=d_scale[:], in_=dict_scale.rearrange("(p t) o -> p (t o)", t=PACK))
        load_dict(0)
        for q in range(4):
            load_gate(q)
            load_w(q)
        load_dict(1)
        load_dict(2)
        nc.sync.dma_start(out=w1_raw[:], in_=w1.rearrange("(p j) c -> p (j c)", j=PACK))
        nc.sync.dma_start(out=z_raw[0][:], in_=z_rows[0])
        nc.sync.dma_start(out=z_raw[1][:], in_=z_rows[1])
        nc.sync.dma_start(
            out=b1_col[:].rearrange("p (g t) -> p g t", t=PACK), in_=b1.rearrange("(g p t) -> p g t", p=P, t=PACK)
        )
        b_rows = b.rearrange("(g a) -> g a", a=A)
        nc.sync.dma_start(out=b_col[0:L, :], in_=b_rows)
        nc.sync.dma_start(out=b_col[L:P, 0 : A - 1], in_=b_rows[:, 1:A])
        for c in range(2, N_CH):
            nc.sync.dma_start(out=z_raw[c][:], in_=z_rows[c])

        d_bf = [new("d_bf%d" % r, (b1e - b0) * BANK, BF16) for r, (b0, b1e) in enumerate(PIECES)]
        d_mx = (new("d_codes", N_BLK * P, U32), new("d_scales", N_BLK * P, U8))
        ws_t = [new("ws_t%d" % g, 4 * BANK, BF16) for g in range(2)]
        ws_mx = (new("ws_codes", H, U32), new("ws_scales", H, U8))
        w1_t = new("w1_t", PACK * H, BF16)
        w1_mx = (new("w1_codes", H, U32), new("w1_scales", H, U8))
        weff = [new("wide", PACK * O, BF16, bufs=2) for g in range(2)]
        weff_mx = [(new("weff_codes%d" % g, O, U32), new("weff_scales%d" % g, O, U8)) for g in range(2)]
        z_mx = [(new("z_codes%d" % c, CH, U32), new("z_scales%d" % c, CH, U8)) for c in range(N_CH)]
        gate = {}
        gated = {}

        def groups_in(blk):
            return min(GPB, L - GPB * blk)

        def sigmoid(q):
            gate[q] = new("gate", 2 * C, F32, bufs=3)
            nc.scalar.activation(out=gate[q][:], in_=s_raw[q][:], func=ACT.Sigmoid)

        def gate_product(q):
            gated[q] = new("gated", 2 * C, BF16, bufs=2)
            nc.vector.tensor_tensor(out=gated[q][:], in0=w_raw[q][:], in1=gate[q][:], op=ALU.mult)

        def turn(rows, index):
            words = rows[:].bitcast(F32)
            acc = bank(index)
            for i in range(2):
                for u in range(2):
                    col = (2 * i + u) * P
                    nc.tensor.transpose(acc[:, col : col + P], words[:, 256 * i + u : 256 * (i + 1) : 2], ident[:])
            return acc

        def turned_out(acc, dst):
            nc.scalar.copy(
                out=dst.bitcast(F32).rearrange("p (i r u) -> p i r u", i=2, u=2),
                in_=acc[:].rearrange("p (i u r) -> p i r u", i=2, u=2),
            )

        d_planes = {}

        def widen(r, slots, on_scalar=False):
            width = piece_cols[r][1] - piece_cols[r][0]
            if r not in d_planes:
                d_planes[r] = new("d_planes", PACK * width, BF16, bufs=2, tag="staged")
            for t in slots:
                cols = slice(t * width, (t + 1) * width)
                codes = d_raw[r][:, cols].bitcast(FP8)
                if on_scalar:
                    nc.scalar.activation(
                        out=d_planes[r][:, cols], in_=codes, func=ACT.Copy, scale=d_scale[:, t : t + 1]
                    )
                else:
                    nc.vector.tensor_scalar(
                        out=d_planes[r][:, cols], in0=codes, scalar1=d_scale[:, t : t + 1], scalar2=None, op0=ALU.mult
                    )

        def interleave_dict(r, blk0, blk1):
            first = PIECES[r][0]
            cols = A * groups_in(blk0)
            c0 = (blk0 - first) * GPB * A
            src = d_planes[r][:].rearrange("p (t n) -> p t n", t=PACK)[:, :, c0 : c0 + (blk1 - blk0) * cols]
            dst = d_bf[r][:].rearrange("p (k x) -> p k x", x=BANK)[:, blk0 - first : blk1 - first, 0 : PACK * cols]
            nc.vector.tensor_copy(
                out=dst.rearrange("p k (n i t) -> p k n t i", i=4, t=PACK),
                in_=src.rearrange("p t (k n i) -> p k n t i", k=blk1 - blk0, i=4),
            )

        def quantize_dict(r):
            b0, b1e = PIECES[r]
            quantize(d_mx[0], d_mx[1], d_bf[r][:], b0 * P, (b1e - b0) * P)

        def expand(g, blk, index, move=nc.scalar.copy):
            acc = bank(index)
            for t in range(PACK):
                matmul(acc[:, t * P : (t + 1) * P], ws_mx, (g * PACK + t) * P, d_mx, blk * P, P, True, True)
            ng = groups_in(blk)
            src = acc[:].rearrange("p (t n) -> p t n", t=PACK)[:, :, 0 : ng * A].rearrange("p t (g a) -> p a g t", a=A)
            dst = weff[g][:].rearrange("p (a g t) -> p a g t", a=A, t=PACK)[:, :, GPB * blk : GPB * blk + ng, :]
            move(out=dst, in_=src)

        def interleave_w1(g):
            nc.vector.tensor_copy(
                out=w1_t[:, g * 2048 : (g + 1) * 2048].rearrange("p (t m i j) -> p m t i j", t=PACK, i=2, j=PACK),
                in_=w1_raw[:]
                .rearrange("p (j c) -> p j c", j=PACK)[:, :, g * 512 : (g + 1) * 512]
                .rearrange("p j (m i t) -> p m t i j", i=2, t=PACK),
            )

        z_t = {}

        def turn_z(c, index):
            acc = turn(z_raw[c], index)
            z_t[c] = new("z_t", 2 * Z, BF16, bufs=3)
            turned_out(acc, z_t[c][:])

        def quantize_z(c):
            quantize(z_mx[c][0], z_mx[c][1], z_t[c][:], 0, CH)

        h_planes = {}
        h_words = {}
        h_mx = {}

        h_acc = {}

        def hidden_matmul(c, q, index):
            h_acc[c, q] = bank(index)
            for i in range(2):
                matmul(h_acc[c, q][:, i * CH : (i + 1) * CH], w1_mx, (2 * q + i) * P, z_mx[c], 0, CH, True, True)

        def hidden_out(c, q):
            g = q // 2
            if q % 2 == 0:
                h_planes[c, g] = new("h_planes", PACK * CH, BF16, bufs=4)
            for i in range(2):
                t = 2 * (q % 2) + i
                nc.scalar.activation(
                    out=h_planes[c, g][:, t * CH : (t + 1) * CH],
                    in_=h_acc[c, q][:, i * CH : (i + 1) * CH],
                    func=ACT.Relu,
                    bias=b1_col[:, 2 * q + i : 2 * q + i + 1],
                )

        def hidden(c, q, index):
            hidden_matmul(c, q, index)
            hidden_out(c, q)

        def interleave_h(c, g, on_gpsimd=False):
            h_words[c, g] = new("h_words%d" % g, PACK * CH, BF16)
            if on_gpsimd:
                nc.gpsimd.tensor_scalar(
                    out=h_words[c, g][:].rearrange("p (n t) -> p n t", t=PACK),
                    in0=h_planes[c, g][:].rearrange("p (t n) -> p n t", t=PACK),
                    scalar1=1.0, scalar2=0.0, op0=ALU.mult, op1=ALU.add,
                )
            else:
                nc.vector.tensor_copy(
                    out=h_words[c, g][:].rearrange("p (n i t) -> p n t i", i=4, t=PACK),
                    in_=h_planes[c, g][:].rearrange("p (t n i) -> p n t i", t=PACK, i=4),
                )

        def quantize_h(c, g):
            h_mx[c, g] = (new("h_codes", CH, U32, bufs=4), new("h_scales", CH, U8, bufs=4))
            quantize(h_mx[c, g][0], h_mx[c, g][1], h_words[c, g][:], 0, CH)

        for r, (b0, b1e) in enumerate(PIECES):
            full = min(b1e, L // GPB) - b0
            blocks = d_bf[r][:].rearrange("p (k x) -> p k x", x=BANK)
            nc.vector.memset(blocks[:, 0:full, PACK * A * GPB :], 0.0)
        nc.vector.memset(d_bf[2][:, 2 * BANK + PACK * A * groups_in(N_BLK - 1) :], 0.0)

        widen(0, range(PACK))
        sigmoid(0)
        interleave_dict(0, 0, 2)
        gate_product(0)
        acc0 = turn(gated[0], 0)
        sigmoid(1)
        sigmoid(2)
        interleave_dict(0, 2, 4)
        gate_product(1)
        acc1 = turn(gated[1], 1)
        turned_out(acc0, ws_t[0][:, 0:1024])
        sigmoid(3)
        quantize_dict(0)
        gate_product(2)
        acc2 = turn(gated[2], 2)
        turned_out(acc1, ws_t[0][:, 1024:2048])
        widen(1, range(0, 2), True)
        widen(2, range(PACK))
        quantize(ws_mx[0], ws_mx[1], ws_t[0][:], 0, 512)
        gate_product(3)
        turned_out(acc2, ws_t[1][:, 0:1024])
        widen(1, range(2, PACK), True)
        for blk in range(0, 2):
            expand(0, blk, 4 + blk)
        acc3 = turn(gated[3], 3)
        turned_out(acc3, ws_t[1][:, 1024:2048])
        for blk in range(2, 4):
            expand(0, blk, 4 + blk)
        interleave_dict(2, 8, 10)
        interleave_dict(2, 10, 11)
        interleave_dict(1, 4, 8)
        quantize_dict(2)
        quantize_dict(1)
        quantize(ws_mx[0], ws_mx[1], ws_t[1][:], 512, 512)
        for blk in range(8, N_BLK):
            expand(0, blk, blk - 8)
        interleave_w1(0)
        interleave_w1(1)
        for blk in range(4, 6):
            expand(0, blk, blk - 1)
        for blk in range(0, 1):
            expand(1, blk, 5 + blk, nc.vector.tensor_copy)
        for blk in range(6, 8):
            expand(0, blk, blk - 6)
        turn_z(0, 2)
        turn_z(1, 3)
        quantize(w1_mx[0], w1_mx[1], w1_t[:], 0, H)
        quantize_z(0)
        quantize_z(1)
        for blk in range(1, 4):
            expand(1, blk, blk + 4)
        for q in range(4):
            hidden(0, q, q)
        quantize(weff_mx[0][0], weff_mx[0][1], weff[0][:, 0:4096], 0, 1024)
        quantize(weff_mx[0][0], weff_mx[0][1], weff[0][:, 4096:5120], 1024, 256)
        for blk in range(4, 7):
            expand(1, blk, blk, nc.vector.tensor_copy)
        interleave_h(0, 0)
        interleave_h(0, 1)
        quantize_h(0, 0)
        quantize_h(0, 1)
        for blk in range(7, N_BLK):
            expand(1, blk, blk % 8)
        hidden(1, 0, 3)
        hidden(1, 1, 4)
        turn_z(2, 5)
        z3_acc = turn(z_raw[3], 7)
        for k in range(XB):
            quantize(weff_mx[1][0], weff_mx[1][1], weff[1][:, k * 1024 : (k + 1) * 1024], k * 256, 256)

        logits = {}
        run_max = {}
        top = {}
        shifted = {}
        expd = {}
        sums = {}
        small = {}
        turned = {}
        staged = {}

        def logits_bank(c, k):
            logits[c, k] = bank(k)
            for i in range(2):
                for g in range(2):
                    matmul(
                        logits[c, k][:, i * CH : (i + 1) * CH], weff_mx[g], (2 * k + i) * P, h_mx[c, g], 0, CH,
                        g == 0, g == 1,
                    )

        def x_of(c, j):
            return logits[c, j // 2][:, (j % 2) * CH : (j % 2 + 1) * CH]

        def bias_of(j):
            return b_col[:, 2 * j : 2 * j + 1]

        def max_start(c):
            for j in range(2):
                run_max[c, j] = new("run_max%d" % j, CH, F32, bufs=2)
                nc.scalar.activation(out=run_max[c, j][:], in_=x_of(c, j), func=ACT.Identity, bias=bias_of(j))

        def max_step(c, j):
            chain = run_max[c, j % 2]
            nc.vector.scalar_tensor_tensor(
                out=chain[:], in0=x_of(c, j), scalar=bias_of(j), in1=chain[:], op0=ALU.add, op1=ALU.max
            )

        def max_join(c):
            small[c, "joined"] = new("joined", CH, F32, bufs=2)
            nc.vector.tensor_tensor(
                out=small[c, "joined"][:], in0=run_max[c, 0][:], in1=run_max[c, 1][:], op=ALU.max
            )

        def max_swap(c):
            small[c, "swapped"] = new("swapped", CH, F32, bufs=2)
            nc.scalar.copy(out=small[c, "swapped"][0:L, :], in_=small[c, "joined"][L:P, :])
            nc.scalar.copy(out=small[c, "swapped"][L:P, :], in_=small[c, "joined"][0:L, :])

        def max_cross(c):
            top[c] = new("top", CH, F32, bufs=2)
            nc.vector.tensor_tensor(out=top[c][:], in0=small[c, "joined"][:], in1=small[c, "swapped"][:], op=ALU.max)
            shifted[c] = new("shifted", PAIRS * CH, F32, bufs=3)
            expd[c] = new("wide", PAIRS * CH, F32, bufs=2)

        def shift(c, j):
            nc.vector.scalar_tensor_tensor(
                out=shifted[c][:, j * CH : (j + 1) * CH], in0=x_of(c, j), scalar=bias_of(j), in1=top[c][:],
                op0=ALU.add, op1=ALU.subtract,
            )

        def exponent(c, k):
            cols = slice(k * BANK, (k + 1) * BANK)
            nc.scalar.activation(out=expd[c][:, cols], in_=shifted[c][:, cols], func=ACT.Exp)

        def add_letters(c, i, j, acc):
            nc.tensor.matmul(
                acc, lhsT=expd[c][:, j * CH + i * P : j * CH + (i + 1) * P],
                rhs=ident[:], start=(j == 0), stop=(j == PAIRS - 1), is_transpose=True,
            )

        def sum_letters(c, i, index):
            if i == 0:
                sums[c] = bank(index)
            for j in range(PAIRS):
                add_letters(c, i, j, sums[c][:, i * P : (i + 1) * P])

        def sum_halves(c, total):
            nc.vector.tensor_reduce(
                out=total.rearrange("p (i g) -> p i g", i=2),
                in_=sums[c][:, 0:CH].rearrange("p (i h g) -> p i g h", i=2, h=2),
                axis=AXIS.X,
                op=ALU.add,
            )

        def logarithm(c0, c1):
            cols = slice(c0 * P, c1 * P)
            nc.scalar.activation(out=lse[:, cols], in_=totals[:, cols], func=ACT.Ln)

        totals = new("totals", N_CH * P, F32)
        lse = new("lse", N_CH * P, F32)

        def pairs_of(part):
            return range(4 * part, min(4 * part + 4, PAIRS))

        def turn_back(c, i, part, acc):
            turned[c, i, part] = acc
            for slot, j in enumerate(pairs_of(part)):
                nc.tensor.transpose(
                    acc[:, slot * P : (slot + 1) * P],
                    shifted[c][:, j * CH + i * P : j * CH + (i + 1) * P], ident[:],
                )

        def staged_of(c):
            if c not in staged:
                staged[c] = new("staged", 2 * O, F32, bufs=2)
            return staged[c][:].rearrange("p (i g a) -> p i g a", i=2, a=A)

        def finish(c, i, part, groups=slice(0, L)):
            letters = 2 * len(pairs_of(part))
            count = groups.stop - groups.start
            first = c * P + i * L
            nc.vector.tensor_tensor(
                out=staged_of(c)[:, i, groups, 8 * part : 8 * part + letters],
                in0=turned[c, i, part].rearrange("p (a g) -> p g a", g=L)[:, groups, :],
                in1=lse[:, first + groups.start : first + groups.stop].unsqueeze(2).to_broadcast([P, count, letters]),
                op=ALU.subtract,
            )

        def finish_ends(c):
            nc.vector.tensor_tensor(
                out=staged_of(c)[:, :, :, 16:A],
                in0=turned[c, "ends"].rearrange("p (i a g) -> p i g a", i=2, g=L),
                in1=lse[:, c * P : (c + 1) * P].rearrange("p (i g) -> p i g", i=2).unsqueeze(3).to_broadcast([P, 2, L, 4]),
                op=ALU.subtract,
            )

        def store(c, i, groups=slice(0, L)):
            cols = slice(groups.start * A, groups.stop * A)
            nc.sync.dma_start(out=out_rows[c, i][:, cols], in_=staged[c][:, i * O + cols.start : i * O + cols.stop])

        def turn_part(c, i, part, index):
            acc = bank(index)
            turn_back(c, i, part, acc[:])

        def turn_ends(c, index):
            acc = bank(index)
            turned[c, "ends"] = acc[:]
            for i in range(2):
                turn_back(c, i, 2, acc[:, i * CH : (i + 1) * CH])

        def reduce_sums(c):
            sum_halves(c, totals[:, c * P : (c + 1) * P])

        def shift_bank(c, k):
            shift(c, 2 * k)
            shift(c, 2 * k + 1)
            exponent(c, k)

        def max_steps(c):
            for j in range(2, PAIRS):
                max_step(c, j)

        logits_bank(0, 0)
        max_start(0)
        logits_bank(0, 1)
        hidden(1, 2, 6)
        hidden(1, 3, 5)
        quantize_z(2)
        z_t[3] = new("z_t", 2 * Z, BF16, bufs=3)
        turned_out(z3_acc, z_t[3][:])
        for k in range(2, XB):
            logits_bank(0, k)
        hidden(2, 0, 6)
        hidden(2, 1, 5)
        hidden_matmul(2, 2, 7)
        hidden_matmul(2, 3, 6)
        max_steps(0)
        interleave_h(1, 0)
        max_join(0)
        max_swap(0)
        interleave_h(1, 1)
        quantize_z(3)
        quantize_h(1, 1)
        max_cross(0)
        quantize_h(1, 0)
        interleave_h(2, 0, True)
        for k in range(XB):
            shift_bank(0, k)
            logits_bank(1, k)
            if k == 1:
                max_start(1)

        hidden_out(2, 2)
        hidden_out(2, 3)
        sum_letters(0, 0, 5)
        sum_letters(0, 1, 5)
        hidden_matmul(3, 0, 7)
        hidden_matmul(3, 1, 6)
        max_steps(1)
        quantize_h(2, 0)
        max_join(1)
        max_swap(1)
        hidden_out(3, 0)
        hidden_out(3, 1)
        interleave_h(3, 0, True)
        interleave_h(2, 1)
        reduce_sums(0)
        max_cross(1)
        quantize_h(2, 1)
        hidden_matmul(3, 2, 5)
        hidden_matmul(3, 3, 7)
        for k in range(XB):
            shift_bank(1, k)
            logits_bank(2, k)
            if k == 1:
                max_start(2)

        hidden_out(3, 2)
        hidden_out(3, 3)
        sum_letters(1, 0, 6)
        sum_letters(1, 1, 6)
        max_steps(2)
        quantize_h(3, 0)
        max_join(2)
        max_swap(2)
        interleave_h(3, 1)
        reduce_sums(1)
        logarithm(0, 2)
        max_cross(2)
        quantize_h(3, 1)

        turn_part(0, 0, 0, 5)
        turn_part(0, 0, 1, 7)
        turn_ends(0, 6)
        for k in range(XB):
            shift_bank(2, k)
            if k < 4:
                logits_bank(3, k)
        turn_part(0, 1, 0, 4)
        max_start(3)
        finish(0, 0, 0)
        turn_part(0, 1, 1, 5)
        finish(0, 0, 1)
        turn_part(1, 0, 0, 7)
        finish_ends(0)
        store(0, 0)
        turn_ends(1, 6)
        finish(0, 1, 0)
        logits_bank(3, 4)
        finish(0, 1, 1)
        store(0, 1)
        turn_part(1, 0, 1, 5)
        finish(1, 0, 0)
        turn_part(1, 1, 0, 7)
        finish_ends(1)
        turn_part(1, 1, 1, 6)
        finish(1, 0, 1)
        store(1, 0)
        sum_letters(2, 0, 5)
        sum_letters(2, 1, 5)
        finish(1, 1, 0)
        turn_part(2, 0, 0, 7)
        finish(1, 1, 1)
        store(1, 1)
        turn_part(2, 0, 1, 6)

        for j in range(2, PAIRS):
            max_step(3, j)
        reduce_sums(2)
        logarithm(2, 3)
        turn_ends(2, 5)
        max_join(3)
        max_swap(3)
        finish(2, 0, 0)
        finish(2, 0, 1)
        max_cross(3)
        turn_part(2, 1, 0, 7)
        turn_part(2, 1, 1, 6)
        for k in range(XB):
            shift_bank(3, k)
        turn_part(3, 0, 0, 0)
        tail_sums = [bank(1 + i) for i in range(2)]
        for j in range(PAIRS):
            for i in range(2):
                add_letters(3, i, j, tail_sums[i][:, 0:P])
        turn_part(3, 0, 1, 3)
        turn_ends(3, 4)
        finish_ends(2)
        store(2, 0)
        turn_part(3, 1, 0, 5)
        finish(2, 1, 0)
        turn_part(3, 1, 1, 7)
        finish(2, 1, 1)
        store(2, 1)
        for i in range(2):
            nc.vector.tensor_reduce(
                out=totals[:, 3 * P + i * L : 3 * P + (i + 1) * L],
                in_=tail_sums[i][:, 0:P].rearrange("p (h g) -> p g h", h=2),
                axis=AXIS.X,
                op=ALU.add,
            )
        logarithm(3, 4)
        for i in range(2):
            for groups in (slice(0, L // 2), slice(L // 2, L)):
                for part in range(3):
                    finish(3, i, part, groups)
                store(3, i, groups)
